import numpy as np
import ml_dtypes


def mxq(x, axis, fmt="e4m3"):
    dtype, down = {"e4m3": (ml_dtypes.float8_e4m3fn, 7), "e5m2": (ml_dtypes.float8_e5m2, 14)}[fmt]
    v = np.moveaxis(np.asarray(x, np.float32).astype(ml_dtypes.bfloat16).astype(np.float64), axis, -1)
    blocks = v.reshape(v.shape[:-1] + (-1, 32))
    amax = np.abs(blocks).max(-1, keepdims=True)
    byte = np.maximum(np.where(amax > 0, np.frexp(amax)[1] - 1 + 127, 0) - down, 1)
    scale = np.exp2(byte - 127.0)
    codes = (blocks / scale).astype(np.float32).astype(dtype).astype(np.float64)
    return np.moveaxis((codes * scale).reshape(v.shape), -1, axis)


WIDE = False


def mx_kscale(k):
    if not WIDE:
        return np.ones(k)
    levels = np.array([10, -10, 5, -5, 0])
    if k % 512:
        return np.exp2(np.random.permutation(np.resize(levels, k // 32))).repeat(32)
    a = np.empty((k // 512, 16))
    for p in range(k // 512):
        a[p, :8] = np.random.permutation(np.resize(levels, 8))
        for g in range(8):
            far = levels[np.abs(levels - a[p, g]) >= 10]
            a[p, g + 8] = far[np.random.randint(len(far))]
    return np.exp2(a.ravel()).repeat(32)


def f64(x):
    return np.asarray(x).astype(np.float64)


def striped(idx):
    return np.tile(idx.reshape(-1, 16).T, (8, 1)).astype(np.uint16)


def unstriped(offs):
    return offs[:16].T.reshape(-1).astype(np.int64)


def pack_weight(w):
    k, n = w.shape
    w = f64(np.asarray(w, np.float32).astype(ml_dtypes.bfloat16)).reshape(k // 32, 32, n)
    amax = np.abs(w).max(1)
    byte = np.clip(np.where(amax > 0, np.frexp(amax)[1] - 1 + 127 - 7, 1), 1, 254)
    scaled = (w * np.exp2(127.0 - byte)[:, None, :]).reshape(k, n).astype(np.float32)
    words = np.ascontiguousarray(scaled.reshape(k // 512, 128, 4, n).transpose(0, 1, 3, 2)).astype(ml_dtypes.float8_e4m3fn).view(np.uint8)
    return words, np.ascontiguousarray(byte.astype(np.uint8).reshape(k // 512, 16, n))


def unpack_weight(words, scales):
    g, p, n, _ = words.shape
    vals = np.ascontiguousarray(words).view(ml_dtypes.float8_e4m3fn).astype(np.float64) * np.repeat(np.exp2(scales.astype(np.float64) - 127.0), 8, axis=1)[..., None]
    return vals.transpose(0, 1, 3, 2).reshape(g * 512, n)


def planes(y):
    n, m = y.shape
    v = y.astype(np.float32).astype(ml_dtypes.bfloat16).astype(np.float64).reshape(n // 32, 32, m)
    top = np.abs(v).max(1)
    byte = np.clip(np.where(top > 0, np.frexp(top)[1] - 1 + 127 - 7, 1), 1, 254)
    codes = (v * np.exp2(127.0 - byte)[:, None, :]).reshape(n, m).astype(np.float32).astype(ml_dtypes.float8_e4m3fn).view(np.uint8)
    words = codes.reshape(n // 512, 128, 4, m).transpose(0, 1, 3, 2)
    return np.ascontiguousarray(words), np.ascontiguousarray(byte.astype(np.uint8).reshape(n // 512, 16, m))


def relu(v):
    return np.maximum(v, 0.0)


K, T, S, J, H, N, W = 1024, 1024, 512, 512, 512, 512, 2048


def setup_inputs():
    n = np.random.standard_normal
    s = mx_kscale(K)[:, None]
    u = mx_kscale(H)
    r = mx_kscale(J)[:, None]
    packed_xT = pack_weight(n((K, T)) * s)
    packed_eT = pack_weight(n((J, W)) * r)
    return {
        "x_words": packed_xT[0],
        "x_scales": packed_xT[1],
        "e_words": packed_eT[0],
        "e_scales": packed_eT[1],
        "w1": (n((K, H)) / np.sqrt(2 * K) / s * u).astype(np.float32),
        "w2": (n((J, H)) / np.sqrt(2 * J) / r * u).astype(np.float32),
        "w3": (n((H, N)) / np.sqrt(H) / u[:, None]).astype(np.float32),
        "bias": (0.3 * n((H, 1)) * u[:, None]).astype(np.float32),
        "offs": striped(np.random.permutation(T)[:S]),
        "item": striped(np.random.permutation(W)[:S]),
    }


def reference(x_words, x_scales, e_words, e_scales, w1, w2, w3, bias, offs, item):
    xq = unpack_weight(x_words, x_scales)[:, unstriped(offs)]
    e_item = unpack_weight(e_words, e_scales)[:, unstriped(item)]
    h = relu((mxq(f64(w1), 0, "e4m3").T @ xq + mxq(f64(w2), 0, "e4m3").T @ e_item) + f64(bias))
    out_0 = mxq(f64(w3), 0, "e4m3").T @ mxq(h, 0, "e4m3")
    return (out_0,) + planes(out_0)

from contextlib import ExitStack

import concourse.mybir as mybir

F32 = mybir.dt.float32
BF16 = mybir.dt.bfloat16
I32 = mybir.dt.int32
U32 = mybir.dt.uint32
U16 = mybir.dt.uint16
U8 = mybir.dt.uint8
FP8X4 = mybir.dt.float8_e4m3fn_x4
ACT = mybir.ActivationFunctionType

P = 128
PACK = 4
K_PASS = P * PACK
PAIRS = 512
WIDTH = 512
CHUNK = 128
CHUNKS = PAIRS // CHUNK
HALF = WIDTH // 2

FLOPS = 2 * (1024 + 512 + 512) * 512 * 512


def tile_picked_zuit_relu_po_kernel(
    tc, x_words, x_scales, e_words, e_scales, w1, w2, w3, bias, offs, item, out_0, out_1, out_2
):
    nc = tc.nc
    with ExitStack() as ctx:
        keep = ctx.enter_context(tc.tile_pool(name="keep", bufs=1))
        psum = ctx.enter_context(tc.psum_pool(name="psum", bufs=1))

        def sb(name, shape, dtype):
            return keep.tile(shape, dtype, name=name, align_bytes=64)

        offs_t = keep.tile([P, PAIRS // 16], U16, name="offs_t")
        item_t = keep.tile([P, PAIRS // 16], U16, name="item_t")
        bias_t = sb("bias_t", [P, PACK], F32)
        x_tab = [sb("x_tab%d" % o, [P, 1024], U32) for o in range(2)]
        e_tab = sb("e_tab", [P, 2048], U32)
        xs_tab = sb("xs_tab", [P, 1024], U8)
        es_tab = sb("es_tab", [P, 2048], U8)
        raw1 = [sb("raw1_%d" % g, [P, PACK, WIDTH], F32) for g in range(2)]
        raw2 = [sb("raw2_%d" % u, [P, PACK, HALF], F32) for u in range(2)]
        raw3 = [sb("raw3_%d" % u, [P, PACK, HALF], F32) for u in range(2)]

        def words_of(table, o):
            return table[o].rearrange("p n t -> p (n t)").bitcast(I32)

        def rows_of(w, g):
            return w[g * K_PASS : (g + 1) * K_PASS, :].rearrange("(p j) c -> p j c", j=PACK)

        nc.gpsimd.memset(xs_tab[:].bitcast(I32), 0)
        nc.gpsimd.memset(es_tab[:].bitcast(I32), 0)
        nc.sync.dma_start(offs_t[:], offs)
        nc.sync.dma_start(x_tab[0][:].bitcast(I32), words_of(x_words, 0))
        for q in range(4):
            nc.sync.dma_start(
                xs_tab[32 * q : 32 * q + 8, :].bitcast(I32), x_scales[:, 4 * q : 4 * q + 4, :].bitcast(I32)
            )
        nc.sync.dma_start(raw1[0][:], rows_of(w1, 0))
        nc.sync.dma_start(x_tab[1][:].bitcast(I32), words_of(x_words, 1))
        nc.sync.dma_start(item_t[:], item)
        for q in range(4):
            nc.sync.dma_start(
                es_tab[32 * q + 8 : 32 * q + 12, :].bitcast(I32), e_scales[0, 4 * q : 4 * q + 4, :].bitcast(I32)
            )
        nc.sync.dma_start(raw1[1][:], rows_of(w1, 1))
        nc.sync.dma_start(e_tab[:].bitcast(I32), words_of(e_words, 0))
        nc.sync.dma_start(bias_t[:], bias.rearrange("(p t) o -> p (t o)", t=PACK))
        for u in range(2):
            nc.sync.dma_start(raw2[u][:], rows_of(w2, 0)[:, :, u * HALF : (u + 1) * HALF])
        for u in range(2):
            nc.sync.dma_start(raw3[u][:], rows_of(w3, 0)[:, :, u * HALF : (u + 1) * HALF])

        w_codes = [sb("w_codes%d" % g, [P, WIDTH], U32) for g in range(4)]
        w_scale = [sb("w_scale%d" % g, [P, WIDTH], U8) for g in range(4)]

        def deal(copy, dst, src, m0, m1):
            copy(
                dst[:, :, m0:m1, :].rearrange("p t m j -> p m j t"),
                src[:, :, PACK * m0 : PACK * m1].rearrange("p j (m t) -> p m j t", t=PACK),
            )

        def quantize(codes, scales, values):
            nc.vector.quantize_mx(out=codes.bitcast(FP8X4), scales=scales, in_=values)

        def cast(name, src, split):
            width = src.shape[2] // PACK
            dst = sb(name, [P, PACK, width, PACK], BF16)
            if split > 0:
                deal(nc.scalar.copy, dst, src, 0, split)
            if split < width:
                deal(nc.vector.tensor_copy, dst, src, split, width)
            return dst

        def quantize_whole(g, dst):
            quantize(w_codes[g][:], w_scale[g][:], dst[:].rearrange("p t m j -> p (t m j)"))

        def quantize_half(g, u, dst):
            for t in range(PACK):
                cols = slice(t * P + u * 64, t * P + (u + 1) * 64)
                quantize(w_codes[g][:, cols], w_scale[g][:, cols], dst[:, t, :, :].rearrange("p m j -> p (m j)"))

        x_g = [sb("x_g%d" % o, [P, PAIRS], U32) for o in range(2)]
        e_g = sb("e_g", [P, PAIRS], U32)
        xs_g = sb("xs_g", [P, PAIRS], U8)
        es_g = sb("es_g", [P, PAIRS], U8)

        acc1 = [psum.tile([P, PACK, CHUNK], F32, name="acc1_%d" % c) for c in range(CHUNKS)]
        acc2 = [psum.tile([P, PACK, CHUNK], F32, name="acc2_%d" % c) for c in range(CHUNKS)]

        def chunk(c):
            return slice(c * CHUNK, (c + 1) * CHUNK)

        def product(g, codes, scales, first, last):
            for c in range(CHUNKS):
                for t in range(PACK):
                    cols = slice(t * P, (t + 1) * P)
                    nc.tensor.matmul_mx(
                        out=acc1[c][:, t, :],
                        lhsT=w_codes[g][:, cols].bitcast(FP8X4),
                        lhsT_scale=w_scale[g][:, cols],
                        rhs=codes[:, chunk(c)].bitcast(FP8X4),
                        rhs_scale=scales[:, chunk(c)],
                        start=(first and t == 0),
                        stop=(last and t == PACK - 1),
                    )

        nc.vector.tensor_copy(x_g[0][:], x_tab[0][:].indirect(offs_t[:]))
        nc.vector.tensor_copy(xs_g[:], xs_tab[:].indirect(offs_t[:]))
        g10 = cast("g10", raw1[0][:], 128)
        nc.vector.tensor_copy(x_g[1][:], x_tab[1][:].indirect(offs_t[:]))
        nc.vector.tensor_copy(es_g[:], es_tab[:].indirect(item_t[:]))
        quantize_whole(0, g10)
        g11 = cast("g11", raw1[1][:], 64)
        quantize_whole(1, g11)
        product(0, x_g[0][:], xs_g[:], True, False)
        nc.vector.tensor_copy(e_g[:], e_tab[:].indirect(item_t[:]))
        product(1, x_g[1][:], xs_g[4:P, :], False, False)
        quantize_half(2, 0, cast("g20", raw2[0][:], 24))
        quantize_half(2, 1, cast("g21", raw2[1][:], 24))
        product(2, e_g[:], es_g[8:P, :], False, True)

        h_rows = [sb("h_rows%d" % c, [P, PACK, CHUNK], BF16) for c in range(CHUNKS)]
        h_grp = [sb("h_grp%d" % c, [P, CHUNK, PACK], BF16) for c in range(CHUNKS)]
        h_codes = [sb("h_codes%d" % c, [P, CHUNK], U32) for c in range(CHUNKS)]
        h_scale = [sb("h_scale%d" % c, [P, CHUNK], U8) for c in range(CHUNKS)]
        y_rows = [sb("y_rows%d" % u, [P, PACK, HALF], F32) for u in range(2)]
        y_grp = [sb("y_grp%d" % c, [P, CHUNK, PACK], BF16) for c in range(CHUNKS)]
        y_codes = sb("y_codes", [P, PAIRS], U32)
        y_scale = sb("y_scale", [P, PAIRS], U8)

        def interleave(dst, src):
            nc.vector.tensor_copy(
                dst.rearrange("p (c i) t -> p c t i", i=4), src.rearrange("p t (c i) -> p c t i", i=4)
            )

        def relu(c):
            for t in range(PACK):
                nc.scalar.activation(h_rows[c][:, t, :], acc1[c][:, t, :], ACT.Relu, bias=bias_t[:, t : t + 1])

        def quantize_h(c):
            quantize(h_codes[c][:], h_scale[c][:], h_grp[c][:].rearrange("p n t -> p (n t)"))

        relu(0)
        relu(1)
        g30 = cast("g30", raw3[0][:], 0)
        interleave(h_grp[0][:], h_rows[0][:])
        quantize_half(3, 0, g30)
        quantize_h(0)
        g31 = cast("g31", raw3[1][:], 0)
        relu(2)
        relu(3)
        interleave(h_grp[1][:], h_rows[1][:])
        quantize_half(3, 1, g31)
        quantize_h(1)
        interleave(h_grp[2][:], h_rows[2][:])
        interleave(h_grp[3][:], h_rows[3][:])
        quantize_h(2)
        quantize_h(3)

        out_rows = out_0.rearrange("(p t) j -> p t j", t=PACK)
        for c in range(CHUNKS):
            u, v = divmod(c, 2)
            for t in range(PACK):
                cols = slice(t * P, (t + 1) * P)
                nc.tensor.matmul_mx(
                    out=acc2[c][:, t, :],
                    lhsT=w_codes[3][:, cols].bitcast(FP8X4),
                    lhsT_scale=w_scale[3][:, cols],
                    rhs=h_codes[c][:].bitcast(FP8X4),
                    rhs_scale=h_scale[c][:],
                    start=True,
                    stop=True,
                )
            nc.scalar.copy(y_rows[u][:, :, chunk(v)], acc2[c][:])
            if v == 1:
                nc.sync.dma_start(out_rows[:, :, u * HALF : (u + 1) * HALF], y_rows[u][:])
        for c in range(CHUNKS + 1):
            if c < CHUNKS:
                u, v = divmod(c, 2)
                interleave(y_grp[c][:], y_rows[u][:, :, chunk(v)])
            if c > 0:
                quantize(y_codes[:, chunk(c - 1)], y_scale[:, chunk(c - 1)], y_grp[c - 1][:].rearrange("p n t -> p (n t)"))
        nc.sync.dma_start(words_of(out_1, 0), y_codes[:].bitcast(I32))
        for q in range(4):
            queue = nc.scalar if q % 2 else nc.sync
            queue.dma_start(out_2[0, 4 * q : 4 * q + 4, :].bitcast(I32), y_scale[32 * q : 32 * q + 4, :].bitcast(I32))
